import numpy as np
import ml_dtypes


def mxq(x, axis, fmt="e4m3"):
    dtype, down = {"e4m3": (ml_dtypes.float8_e4m3fn, 7), "e5m2": (ml_dtypes.float8_e5m2, 14)}[fmt]
    v = np.moveaxis(np.asarray(x, np.float32).astype(ml_dtypes.bfloat16).astype(np.float64), axis, -1)
    blocks = v.reshape(v.shape[:-1] + (-1, 32))
    amax = np.abs(blocks).max(-1, keepdims=True)
    byte = np.maximum(np.where(amax > 0, np.frexp(amax)[1] - 1 + 127, 0) - down, 1)
    scale = np.exp2(byte - 127.0)
    codes = (blocks / scale).astype(np.float32).astype(dtype).astype(np.float64)
    return np.moveaxis((codes * scale).reshape(v.shape), -1, axis)


WIDE = False


def mx_kscale(k):
    if not WIDE:
        return np.ones(k)
    levels = np.array([10, -10, 5, -5, 0])
    if k % 512:
        return np.exp2(np.random.permutation(np.resize(levels, k // 32))).repeat(32)
    a = np.empty((k // 512, 16))
    for p in range(k // 512):
        a[p, :8] = np.random.permutation(np.resize(levels, 8))
        for g in range(8):
            far = levels[np.abs(levels - a[p, g]) >= 10]
            a[p, g + 8] = far[np.random.randint(len(far))]
    return np.exp2(a.ravel()).repeat(32)


def f64(x):
    return np.asarray(x).astype(np.float64)


def striped(idx):
    return np.tile(idx.reshape(-1, 16).T, (8, 1)).astype(np.uint16)


def unstriped(offs):
    return offs[:16].T.reshape(-1).astype(np.int64)


K, T, E, C, N = 2048, 512, 4, 128, 128


def by_expert(wq, xq):
    return np.concatenate([wq[e].T @ xq[:, e * C:(e + 1) * C] for e in range(E)], axis=1)


def setup_inputs():
    n = np.random.standard_normal
    s = mx_kscale(K)[:, None]
    return {
        "xT": (n((K, T)) * s).astype(np.float32),
        "w": (n((E, K, N)) / np.sqrt(K) / s[None]).astype(np.float32),
        "gate": np.tile(np.random.uniform(0.2, 1.0, E * C), (N, 1)).astype(np.float32),
        "offs": striped(np.random.permutation(T)[:E * C]),
    }


def reference(xT, w, gate, offs):
    idx = unstriped(offs)
    xq = mxq(f64(xT)[:, idx], 0, "e4m3")
    y = by_expert(mxq(f64(w), 1, "e4m3"), xq)
    out = np.zeros((N, T))
    out[:, idx] = f64(gate) * y
    return out

@@ -1,0 +1,229 @@
+from contextlib import ExitStack
+
+import concourse.mybir as mybir
+
+K, T, E, C, N = 2048, 512, 4, 128, 128
+FLOPS = 2 * K * N * E * C
+
+F32 = mybir.dt.float32
+BF16 = mybir.dt.bfloat16
+U32 = mybir.dt.uint32
+U16 = mybir.dt.uint16
+U8 = mybir.dt.uint8
+I32 = mybir.dt.int32
+FP8X4 = mybir.dt.float8_e4m3fn_x4
+
+P = 128
+PASSES = K // 512
+S = E * C
+
+V_ORDER = [0, 1, 2, 3, 4, 5, 6, 7]
+S_BASE = {3: 0, 1: 1024}
+
+
+def tile_routed_moe_kernel(tc, xT, w, gate, offs, out):
+    nc = tc.nc
+    mult = mybir.AluOpType.mult
+    add = mybir.AluOpType.add
+    copy_fn = mybir.ActivationFunctionType.Copy
+
+    with ExitStack() as ctx:
+        keep = ctx.enter_context(tc.tile_pool(name="keep", bufs=1))
+        psum = ctx.enter_context(tc.psum_pool(name="psum", bufs=1))
+
+        offsets = keep.tile([P, S // 16], U16, name="offsets")
+        nc.sync.dma_start(offsets[:], offs)
+
+        warm_in = keep.tile([P, 8], F32, name="warm_in")
+        warm_out = keep.tile([P, 8], F32, name="warm_out")
+        nc.vector.memset(warm_in[:], 0.0)
+        nc.scalar.copy(out=warm_out[:], in_=warm_in[:])
+
+        x_view = xT.rearrange("(g p u e) n -> g u p e n", p=P, u=2, e=2)
+        x_raw = {}
+        for i in range(2 * PASSES):
+            x_raw[i] = keep.tile([P, 2, T], F32, name="xraw%d" % i)
+            nc.sync.dma_start(out=x_raw[i][:], in_=x_view[i // 2, i % 2])
+
+        w_view = w.rearrange("e (g p j) n -> e p g (j n)", p=P, j=4)
+        w_raw = {}
+        for e in range(E):
+            w_raw[e] = keep.tile([P, PASSES, 4 * N], F32, name="wraw%d" % e)
+        gate_sb = keep.tile([P, S], F32, name="gate_sb")
+        nc.sync.dma_start(out=w_raw[0][:], in_=w_view[0])
+        nc.sync.dma_start(out=w_raw[1][:], in_=w_view[1])
+        nc.sync.dma_start(out=gate_sb[:], in_=gate)
+        nc.sync.dma_start(out=w_raw[2][:], in_=w_view[2])
+        nc.sync.dma_start(out=w_raw[3][:, 0:2], in_=w_view[3][:, 0:2])
+        nc.sync.dma_start(out=w_raw[3][:, 2:3], in_=w_view[3][:, 2:3])
+        nc.sync.dma_start(out=w_raw[3][:, 3:4], in_=w_view[3][:, 3:4])
+
+        vwin = keep.tile([P, len(V_ORDER) * 2 * T], BF16, name="vwin")
+        swin = keep.tile([P, 4 * T], BF16, name="swin")
+        grouped = {}
+        x_codes = {}
+        x_scales = {}
+        big_grouped = {}
+        big_codes = {}
+        big_scales = {}
+        for d in range(PASSES // 2):
+            big_grouped[d] = keep.tile([P, 8 * S], BF16, name="xgrp%d" % d, align_bytes=64)
+            big_codes[d] = keep.tile([P, 2 * S], U32, name="xcodes%d" % d, align_bytes=64)
+            big_scales[d] = keep.tile([P, 2 * S], U8, name="xscales%d" % d, align_bytes=64)
+        flat = {}
+        for d in range(PASSES // 2):
+            flat[d] = keep.tile([P, 4 * S], U32, name="flat%d" % d)
+        for g in range(PASSES):
+            grouped[g] = big_grouped[g // 2][:, (g % 2) * 4 * S : (g % 2 + 1) * 4 * S]
+            x_codes[g] = big_codes[g // 2][:, (g % 2) * S : (g % 2 + 1) * S]
+            x_scales[g] = big_scales[g // 2][:, (g % 2) * S : (g % 2 + 1) * S]
+        w_grouped = {}
+        w_codes = {}
+        w_scales = {}
+        wg01 = keep.tile([P, 2 * PASSES * 4 * N], BF16, name="wgrp01", align_bytes=64)
+        wc01 = keep.tile([P, 2 * PASSES * N], U32, name="wcodes01", align_bytes=64)
+        ws01 = keep.tile([P, 2 * PASSES * N], U8, name="wscales01", align_bytes=64)
+        for e in range(2):
+            w_grouped[e] = wg01[:, e * PASSES * 4 * N : (e + 1) * PASSES * 4 * N]
+            w_codes[e] = wc01[:, e * PASSES * N : (e + 1) * PASSES * N]
+            w_scales[e] = ws01[:, e * PASSES * N : (e + 1) * PASSES * N]
+        for e in range(2, E):
+            w_grouped[e] = keep.tile([P, PASSES * 4 * N], BF16, name="wgrp%d" % e, align_bytes=64)
+            w_codes[e] = keep.tile([P, PASSES * N], U32, name="wcodes%d" % e, align_bytes=64)
+            w_scales[e] = keep.tile([P, PASSES * N], U8, name="wscales%d" % e, align_bytes=64)
+        window = keep.tile([P, T], F32, name="window")
+
+        def cast(eng, dst, src):
+            if eng == "v":
+                nc.vector.tensor_copy(out=dst, in_=src)
+            elif eng == "s":
+                nc.scalar.copy(out=dst, in_=src)
+            else:
+                nc.gpsimd.tensor_scalar(out=dst, in0=src, scalar1=1.0, scalar2=0.0, op0=mult, op1=add)
+
+        def pos(i):
+            return len(V_ORDER) - 1 - V_ORDER.index(i)
+
+        def cast_pairs(i, eng):
+            dst = vwin[:, pos(i) * 2 * T : (pos(i) + 1) * 2 * T].rearrange("p (n e) -> p n e", e=2)
+            cast(eng, dst, x_raw[i][:].rearrange("p e n -> p n e"))
+
+        def gather_v(i):
+            words = flat[i // 4][:, (i % 4) * S : (i % 4 + 1) * S]
+            vw = vwin[:].bitcast(U32)
+            c0 = pos(i) * T
+            if pos(i) == len(V_ORDER) - 1:
+                for h in range(2):
+                    nc.vector.tensor_copy(
+                        out=words[:, h * 256 : (h + 1) * 256],
+                        in_=vw[:, c0 : c0 + T].indirect(offsets[:, h * 16 : (h + 1) * 16]),
+                    )
+            else:
+                nc.vector.tensor_copy(out=words, in_=vw[:, c0 : c0 + 2 * T].indirect(offsets[:]))
+
+        def cast_planes(i, eng):
+            cast(eng, swin[:, S_BASE[i] : S_BASE[i] + 2 * T], x_raw[i][:].rearrange("p e n -> p (e n)"))
+
+        def gather_s(i):
+            g4 = grouped[i // 2][:].rearrange("p (s t) -> p s t", t=4)
+            for e2 in range(2):
+                t = 2 * (i % 2) + e2
+                c0 = S_BASE[i] + e2 * T
+                if c0 + 2 * T <= 4 * T:
+                    nc.scalar.activation(out=g4[:, :, t], in_=swin[:, c0 : c0 + 2 * T].indirect(offsets[:]), func=copy_fn)
+                else:
+                    for h in range(2):
+                        nc.scalar.activation(
+                            out=g4[:, h * 256 : (h + 1) * 256, t],
+                            in_=swin[:, c0 : c0 + T].indirect(offsets[:, h * 16 : (h + 1) * 16]),
+                            func=copy_fn,
+                        )
+
+        def weave(d):
+            nc.vector.tensor_copy(
+                out=big_grouped[d][:].bitcast(I32).rearrange("p (g s u) -> p g s u", g=2, u=2),
+                in_=flat[d][:].bitcast(I32).rearrange("p (g u s) -> p g s u", g=2, u=2),
+            )
+
+        def quant_x(d):
+            nc.vector.quantize_mx(out=big_codes[d][:].bitcast(FP8X4), scales=big_scales[d][:], in_=big_grouped[d][:])
+
+        def cast_w(e, g0, g1, eng):
+            dst = w_grouped[e][:].rearrange("p (g c i j) -> p g c j i", g=PASSES, i=4, j=4)
+            src = w_raw[e][:].rearrange("p g (j c i) -> p g c j i", j=4, i=4)
+            cast(eng, dst[:, g0:g1], src[:, g0:g1])
+
+        def quant_w(e, g0, g1):
+            nc.vector.quantize_mx(
+                out=w_codes[e][:, g0 * N : g1 * N].bitcast(FP8X4),
+                scales=w_scales[e][:, g0 * N : g1 * N],
+                in_=w_grouped[e][:, g0 * 4 * N : g1 * 4 * N],
+            )
+
+        def mm(e, g, acc):
+            nc.tensor.matmul_mx(
+                out=acc,
+                lhsT=w_codes[e][:, g * N : (g + 1) * N].bitcast(FP8X4),
+                lhsT_scale=w_scales[e][:, g * N : (g + 1) * N],
+                rhs=x_codes[g][:, e * C : (e + 1) * C].bitcast(FP8X4),
+                rhs_scale=x_scales[g][:, e * C : (e + 1) * C],
+                start=(g == 0),
+                stop=(g == PASSES - 1),
+            )
+
+        def back(acc, s0, n, name):
+            y = keep.tile([P, n], F32, name=name)
+            nc.scalar.copy(out=y[:], in_=acc[:])
+            nc.vector.tensor_tensor(
+                out=window[:].indirect(offsets[:, s0 // 16 : (s0 + n) // 16]),
+                in0=y[:],
+                in1=gate_sb[:, s0 : s0 + n],
+                op=mult,
+            )
+
+        cast_pairs(0, "v")
+        cast_pairs(1, "s")
+        gather_v(0)
+        cast_pairs(2, "s")
+        gather_v(1)
+        cast_pairs(3, "s")
+        gather_v(2)
+        cast_pairs(4, "s")
+        gather_v(3)
+        cast_pairs(5, "s")
+        weave(0)
+        gather_v(4)
+        quant_x(0)
+        cast_pairs(6, "s")
+        gather_v(5)
+        cast_pairs(7, "s")
+        gather_v(6)
+        gather_v(7)
+        weave(1)
+        cast_w(0, 0, 2, "s")
+        cast_w(0, 2, 4, "s")
+        cast_w(1, 0, 2, "s")
+        cast_w(1, 2, 4, "s")
+        quant_x(1)
+        nc.vector.quantize_mx(out=wc01[:].bitcast(FP8X4), scales=ws01[:], in_=wg01[:])
+
+        acc01 = psum.tile([P, 2 * C], F32, name="acc01")
+        acc2 = psum.tile([P, C], F32, name="acc2")
+        acc3 = psum.tile([P, C], F32, name="acc3")
+        for e in range(2):
+            for g in range(PASSES):
+                mm(e, g, acc01[:, e * C : (e + 1) * C])
+        cast_w(2, 0, 2, "s")
+        cast_w(2, 2, 4, "v")
+        quant_w(2, 0, 4)
+        for g in range(PASSES):
+            mm(2, g, acc2[:])
+        back(acc01, 0, 2 * C, "y01")
+        cast_w(3, 0, 2, "s")
+        cast_w(3, 2, 4, "v")
+        quant_w(3, 0, 4)
+        for g in range(PASSES):
+            mm(3, g, acc3[:])
+        back(acc2, 2 * C, C, "y2")
+        back(acc3, 3 * C, C, "y3")
+        nc.sync.dma_start(out=out, in_=window[:])

@@ -16,103 +16,99 @@ FP8X4 = mybir.dt.float8_e4m3fn_x4
 P = 128
 PASSES = K // 512
 S = E * C
-
-V_ORDER = [0, 1, 2, 3, 4, 5, 6, 7]
-S_BASE = {3: 0, 1: 1024}
+PAIRS = 2 * PASSES
 
 
 def tile_routed_moe_kernel(tc, xT, w, gate, offs, out):
     nc = tc.nc
     mult = mybir.AluOpType.mult
-    add = mybir.AluOpType.add
-    copy_fn = mybir.ActivationFunctionType.Copy
 
     with ExitStack() as ctx:
         keep = ctx.enter_context(tc.tile_pool(name="keep", bufs=1))
         psum = ctx.enter_context(tc.psum_pool(name="psum", bufs=1))
 
         offsets = keep.tile([P, S // 16], U16, name="offsets")
-        nc.sync.dma_start(offsets[:], offs)
-
         warm_in = keep.tile([P, 8], F32, name="warm_in")
         warm_out = keep.tile([P, 8], F32, name="warm_out")
         nc.vector.memset(warm_in[:], 0.0)
         nc.scalar.copy(out=warm_out[:], in_=warm_in[:])
 
         x_view = xT.rearrange("(g p u e) n -> g u p e n", p=P, u=2, e=2)
-        x_raw = {}
-        for i in range(2 * PASSES):
-            x_raw[i] = keep.tile([P, 2, T], F32, name="xraw%d" % i)
-            nc.sync.dma_start(out=x_raw[i][:], in_=x_view[i // 2, i % 2])
-
         w_view = w.rearrange("e (g p j) n -> e p g (j n)", p=P, j=4)
+        x_raw = {}
+        for i in range(PAIRS):
+            x_raw[i] = keep.tile([P, 2, T], F32, name="xraw%d" % i, align_bytes=64)
         w_raw = {}
         for e in range(E):
-            w_raw[e] = keep.tile([P, PASSES, 4 * N], F32, name="wraw%d" % e)
+            for h in range(2):
+                w_raw[(e, h)] = keep.tile([P, 2, 4 * N], F32, name="wraw%d%d" % (e, h), align_bytes=64)
         gate_sb = keep.tile([P, S], F32, name="gate_sb")
-        nc.sync.dma_start(out=w_raw[0][:], in_=w_view[0])
-        nc.sync.dma_start(out=w_raw[1][:], in_=w_view[1])
-        nc.sync.dma_start(out=gate_sb[:], in_=gate)
-        nc.sync.dma_start(out=w_raw[2][:], in_=w_view[2])
-        nc.sync.dma_start(out=w_raw[3][:, 0:2], in_=w_view[3][:, 0:2])
-        nc.sync.dma_start(out=w_raw[3][:, 2:3], in_=w_view[3][:, 2:3])
-        nc.sync.dma_start(out=w_raw[3][:, 3:4], in_=w_view[3][:, 3:4])
 
-        vwin = keep.tile([P, len(V_ORDER) * 2 * T], BF16, name="vwin")
-        swin = keep.tile([P, 4 * T], BF16, name="swin")
-        grouped = {}
+        def load_offs():
+            nc.sync.dma_start(offsets[:], offs)
+
+        def load_x(i):
+            nc.sync.dma_start(out=x_raw[i][:], in_=x_view[i // 2, i % 2])
+
+        def load_x_half(i, h):
+            nc.sync.dma_start(out=x_raw[i][:, :, h * 256 : (h + 1) * 256], in_=x_view[i // 2, i % 2][:, :, h * 256 : (h + 1) * 256])
+
+        def load_w(e, g0, g1):
+            nc.sync.dma_start(out=w_raw[(e, g0 // 2)][:, g0 % 2 : g0 % 2 + g1 - g0], in_=w_view[e][:, g0:g1])
+
+        def load_gate():
+            nc.sync.dma_start(out=gate_sb[:], in_=gate)
+
+        load_offs()
+        for i in range(PAIRS):
+            load_x(i)
+        load_w(0, 0, 2)
+        load_w(0, 2, 4)
+        load_w(1, 0, 2)
+        load_w(1, 2, 4)
+        load_gate()
+        load_w(2, 0, 2)
+        load_w(2, 2, 4)
+        load_w(3, 0, 2)
+        load_w(3, 2, 3)
+        load_w(3, 3, 4)
+
+        vwin = keep.tile([P, PAIRS * 2 * T], BF16, name="vwin")
+        flat = {}
+        for d in range(2):
+            flat[d] = keep.tile([P, 4 * S], U32, name="flat%d" % d)
+        x_grouped = {}
         x_codes = {}
         x_scales = {}
-        big_grouped = {}
-        big_codes = {}
-        big_scales = {}
-        for d in range(PASSES // 2):
-            big_grouped[d] = keep.tile([P, 8 * S], BF16, name="xgrp%d" % d, align_bytes=64)
-            big_codes[d] = keep.tile([P, 2 * S], U32, name="xcodes%d" % d, align_bytes=64)
-            big_scales[d] = keep.tile([P, 2 * S], U8, name="xscales%d" % d, align_bytes=64)
-        flat = {}
-        for d in range(PASSES // 2):
-            flat[d] = keep.tile([P, 4 * S], U32, name="flat%d" % d)
-        for g in range(PASSES):
-            grouped[g] = big_grouped[g // 2][:, (g % 2) * 4 * S : (g % 2 + 1) * 4 * S]
-            x_codes[g] = big_codes[g // 2][:, (g % 2) * S : (g % 2 + 1) * S]
-            x_scales[g] = big_scales[g // 2][:, (g % 2) * S : (g % 2 + 1) * S]
+        for d in range(2):
+            x_scales[d] = keep.tile([P, 2 * S], U8, name="xscales%d" % d, align_bytes=64)
         w_grouped = {}
         w_codes = {}
         w_scales = {}
-        wg01 = keep.tile([P, 2 * PASSES * 4 * N], BF16, name="wgrp01", align_bytes=64)
-        wc01 = keep.tile([P, 2 * PASSES * N], U32, name="wcodes01", align_bytes=64)
-        ws01 = keep.tile([P, 2 * PASSES * N], U8, name="wscales01", align_bytes=64)
-        for e in range(2):
-            w_grouped[e] = wg01[:, e * PASSES * 4 * N : (e + 1) * PASSES * 4 * N]
-            w_codes[e] = wc01[:, e * PASSES * N : (e + 1) * PASSES * N]
-            w_scales[e] = ws01[:, e * PASSES * N : (e + 1) * PASSES * N]
-        for e in range(2, E):
-            w_grouped[e] = keep.tile([P, PASSES * 4 * N], BF16, name="wgrp%d" % e, align_bytes=64)
-            w_codes[e] = keep.tile([P, PASSES * N], U32, name="wcodes%d" % e, align_bytes=64)
-            w_scales[e] = keep.tile([P, PASSES * N], U8, name="wscales%d" % e, align_bytes=64)
+        for q in range(2):
+            w_grouped[q] = keep.tile([P, 2 * PASSES * 4 * N], BF16, name="wgrp%d" % q, align_bytes=64)
+            w_codes[q] = keep.tile([P, 2 * PASSES * N], U32, name="wcodes%d" % q, align_bytes=64)
+            w_scales[q] = keep.tile([P, 2 * PASSES * N], U8, name="wscales%d" % q, align_bytes=64)
         window = keep.tile([P, T], F32, name="window")
 
         def cast(eng, dst, src):
             if eng == "v":
                 nc.vector.tensor_copy(out=dst, in_=src)
-            elif eng == "s":
-                nc.scalar.copy(out=dst, in_=src)
             else:
-                nc.gpsimd.tensor_scalar(out=dst, in0=src, scalar1=1.0, scalar2=0.0, op0=mult, op1=add)
+                nc.scalar.copy(out=dst, in_=src)
 
         def pos(i):
-            return len(V_ORDER) - 1 - V_ORDER.index(i)
+            return PAIRS - 1 - i
 
-        def cast_pairs(i, eng):
+        def cast_pairs(i, eng, n0=0, n1=T):
             dst = vwin[:, pos(i) * 2 * T : (pos(i) + 1) * 2 * T].rearrange("p (n e) -> p n e", e=2)
-            cast(eng, dst, x_raw[i][:].rearrange("p e n -> p n e"))
+            cast(eng, dst[:, n0:n1], x_raw[i][:, :, n0:n1].rearrange("p e n -> p n e"))
 
         def gather_v(i):
             words = flat[i // 4][:, (i % 4) * S : (i % 4 + 1) * S]
             vw = vwin[:].bitcast(U32)
             c0 = pos(i) * T
-            if pos(i) == len(V_ORDER) - 1:
+            if i == 0:
                 for h in range(2):
                     nc.vector.tensor_copy(
                         out=words[:, h * 256 : (h + 1) * 256],
@@ -121,58 +117,49 @@ def tile_routed_moe_kernel(tc, xT, w, gate, offs, out):
             else:
                 nc.vector.tensor_copy(out=words, in_=vw[:, c0 : c0 + 2 * T].indirect(offsets[:]))
 
-        def cast_planes(i, eng):
-            cast(eng, swin[:, S_BASE[i] : S_BASE[i] + 2 * T], x_raw[i][:].rearrange("p e n -> p (e n)"))
-
-        def gather_s(i):
-            g4 = grouped[i // 2][:].rearrange("p (s t) -> p s t", t=4)
-            for e2 in range(2):
-                t = 2 * (i % 2) + e2
-                c0 = S_BASE[i] + e2 * T
-                if c0 + 2 * T <= 4 * T:
-                    nc.scalar.activation(out=g4[:, :, t], in_=swin[:, c0 : c0 + 2 * T].indirect(offsets[:]), func=copy_fn)
-                else:
-                    for h in range(2):
-                        nc.scalar.activation(
-                            out=g4[:, h * 256 : (h + 1) * 256, t],
-                            in_=swin[:, c0 : c0 + T].indirect(offsets[:, h * 16 : (h + 1) * 16]),
-                            func=copy_fn,
-                        )
-
-        def weave(d):
+        def weave(d, tag):
+            x_grouped[d] = keep.tile([P, 8 * S], BF16, name="xgrp%d" % d, tag=tag, align_bytes=64)
             nc.vector.tensor_copy(
-                out=big_grouped[d][:].bitcast(I32).rearrange("p (g s u) -> p g s u", g=2, u=2),
+                out=x_grouped[d][:].bitcast(I32).rearrange("p (g s u) -> p g s u", g=2, u=2),
                 in_=flat[d][:].bitcast(I32).rearrange("p (g u s) -> p g s u", g=2, u=2),
             )
 
-        def quant_x(d):
-            nc.vector.quantize_mx(out=big_codes[d][:].bitcast(FP8X4), scales=big_scales[d][:], in_=big_grouped[d][:])
+        def quant_x(d, tag):
+            x_codes[d] = keep.tile([P, 2 * S], U32, name="xcodes%d" % d, tag=tag, align_bytes=64)
+            nc.vector.quantize_mx(out=x_codes[d][:].bitcast(FP8X4), scales=x_scales[d][:], in_=x_grouped[d][:])
 
         def cast_w(e, g0, g1, eng):
-            dst = w_grouped[e][:].rearrange("p (g c i j) -> p g c j i", g=PASSES, i=4, j=4)
-            src = w_raw[e][:].rearrange("p g (j c i) -> p g c j i", j=4, i=4)
-            cast(eng, dst[:, g0:g1], src[:, g0:g1])
+            b = (e % 2) * PASSES
+            dst = w_grouped[e // 2][:].rearrange("p (g c i j) -> p g c j i", g=2 * PASSES, i=4, j=4)
+            src = w_raw[(e, g0 // 2)][:].rearrange("p g (j c i) -> p g c j i", j=4, i=4)
+            cast(eng, dst[:, b + g0 : b + g1], src[:, g0 % 2 : g0 % 2 + g1 - g0])
 
-        def quant_w(e, g0, g1):
+        def quant_w(e0, e1):
+            q = e0 // 2
+            a = (e0 % 2) * PASSES
+            b = (e1 - 2 * q) * PASSES
             nc.vector.quantize_mx(
-                out=w_codes[e][:, g0 * N : g1 * N].bitcast(FP8X4),
-                scales=w_scales[e][:, g0 * N : g1 * N],
-                in_=w_grouped[e][:, g0 * 4 * N : g1 * 4 * N],
+                out=w_codes[q][:, a * N : b * N].bitcast(FP8X4),
+                scales=w_scales[q][:, a * N : b * N],
+                in_=w_grouped[q][:, a * 4 * N : b * 4 * N],
             )
 
-        def mm(e, g, acc):
-            nc.tensor.matmul_mx(
-                out=acc,
-                lhsT=w_codes[e][:, g * N : (g + 1) * N].bitcast(FP8X4),
-                lhsT_scale=w_scales[e][:, g * N : (g + 1) * N],
-                rhs=x_codes[g][:, e * C : (e + 1) * C].bitcast(FP8X4),
-                rhs_scale=x_scales[g][:, e * C : (e + 1) * C],
-                start=(g == 0),
-                stop=(g == PASSES - 1),
-            )
+        def mm(e, acc):
+            for g in range(PASSES):
+                c0 = ((e % 2) * PASSES + g) * N
+                r0 = (g % 2) * S + e * C
+                nc.tensor.matmul_mx(
+                    out=acc,
+                    lhsT=w_codes[e // 2][:, c0 : c0 + N].bitcast(FP8X4),
+                    lhsT_scale=w_scales[e // 2][:, c0 : c0 + N],
+                    rhs=x_codes[g // 2][:, r0 : r0 + C].bitcast(FP8X4),
+                    rhs_scale=x_scales[g // 2][:, r0 : r0 + C],
+                    start=(g == 0),
+                    stop=(g == PASSES - 1),
+                )
 
-        def back(acc, s0, n, name):
-            y = keep.tile([P, n], F32, name=name)
+        def back(acc, s0, n, name, tag):
+            y = keep.tile([P, n], F32, name=name, tag=tag, align_bytes=64)
             nc.scalar.copy(out=y[:], in_=acc[:])
             nc.vector.tensor_tensor(
                 out=window[:].indirect(offsets[:, s0 // 16 : (s0 + n) // 16]),
@@ -180,6 +167,9 @@ def tile_routed_moe_kernel(tc, xT, w, gate, offs, out):
                 in1=gate_sb[:, s0 : s0 + n],
                 op=mult,
             )
+
+        acc01 = psum.tile([P, 2 * C], F32, name="acc01")
+        acc23 = psum.tile([P, 2 * C], F32, name="acc23")
 
         cast_pairs(0, "v")
         cast_pairs(1, "s")
@@ -191,39 +181,32 @@ def tile_routed_moe_kernel(tc, xT, w, gate, offs, out):
         cast_pairs(4, "s")
         gather_v(3)
         cast_pairs(5, "s")
-        weave(0)
         gather_v(4)
-        quant_x(0)
-        cast_pairs(6, "s")
+        weave(0, "xraw5")
         gather_v(5)
-        cast_pairs(7, "s")
+        cast_pairs(6, "s")
         gather_v(6)
+        cast_pairs(7, "s")
         gather_v(7)
-        weave(1)
         cast_w(0, 0, 2, "s")
+        quant_x(0, "wraw00")
         cast_w(0, 2, 4, "s")
+        weave(1, "wraw01")
         cast_w(1, 0, 2, "s")
+        quant_x(1, "wraw10")
         cast_w(1, 2, 4, "s")
-        quant_x(1)
-        nc.vector.quantize_mx(out=wc01[:].bitcast(FP8X4), scales=ws01[:], in_=wg01[:])
-
-        acc01 = psum.tile([P, 2 * C], F32, name="acc01")
-        acc2 = psum.tile([P, C], F32, name="acc2")
-        acc3 = psum.tile([P, C], F32, name="acc3")
-        for e in range(2):
-            for g in range(PASSES):
-                mm(e, g, acc01[:, e * C : (e + 1) * C])
+        quant_w(0, 2)
+        mm(0, acc01[:, 0:C])
+        mm(1, acc01[:, C : 2 * C])
         cast_w(2, 0, 2, "s")
-        cast_w(2, 2, 4, "v")
-        quant_w(2, 0, 4)
-        for g in range(PASSES):
-            mm(2, g, acc2[:])
-        back(acc01, 0, 2 * C, "y01")
+        cast_w(2, 2, 4, "s")
         cast_w(3, 0, 2, "s")
+        quant_w(2, 3)
+        mm(2, acc23[:, 0:C])
         cast_w(3, 2, 4, "v")
-        quant_w(3, 0, 4)
-        for g in range(PASSES):
-            mm(3, g, acc3[:])
-        back(acc2, 2 * C, C, "y2")
-        back(acc3, 3 * C, C, "y3")
+        quant_w(3, 4)
+        mm(3, acc23[:, C : 2 * C])
+        back(acc01, 0, 2 * C, "y01", "wraw31")
+        back(acc23, 2 * C, 2 * C, "y23", "y23")
+
         nc.sync.dma_start(out=out, in_=window[:])

@@ -59,8 +59,10 @@ def tile_routed_moe_kernel(tc, xT, w, gate, offs, out):
         def load_gate():
             nc.sync.dma_start(out=gate_sb[:], in_=gate)
 
+        load_x_half(0, 0)
         load_offs()
-        for i in range(PAIRS):
+        load_x_half(0, 1)
+        for i in range(1, PAIRS):
             load_x(i)
         load_w(0, 0, 2)
         load_w(0, 2, 4)
@@ -144,8 +146,8 @@ def tile_routed_moe_kernel(tc, xT, w, gate, offs, out):
                 in_=w_grouped[q][:, a * 4 * N : b * 4 * N],
             )
 
-        def mm(e, acc):
-            for g in range(PASSES):
+        def mm(e, acc, g0=0, g1=PASSES):
+            for g in range(g0, g1):
                 c0 = ((e % 2) * PASSES + g) * N
                 r0 = (g % 2) * S + e * C
                 nc.tensor.matmul_mx(
@@ -158,9 +160,11 @@ def tile_routed_moe_kernel(tc, xT, w, gate, offs, out):
                     stop=(g == PASSES - 1),
                 )
 
-        def back(acc, s0, n, name, tag):
+        def back(accs, s0, n, name, tag):
             y = keep.tile([P, n], F32, name=name, tag=tag, align_bytes=64)
-            nc.scalar.copy(out=y[:], in_=acc[:])
+            m = n // len(accs)
+            for a, acc in enumerate(accs):
+                nc.scalar.copy(out=y[:, a * m : (a + 1) * m], in_=acc[:])
             nc.vector.tensor_tensor(
                 out=window[:].indirect(offsets[:, s0 // 16 : (s0 + n) // 16]),
                 in0=y[:],
@@ -168,10 +172,12 @@ def tile_routed_moe_kernel(tc, xT, w, gate, offs, out):
                 op=mult,
             )
 
-        acc01 = psum.tile([P, 2 * C], F32, name="acc01")
+        acc0 = psum.tile([P, C], F32, name="acc0")
+        acc1 = psum.tile([P, C], F32, name="acc1")
         acc23 = psum.tile([P, 2 * C], F32, name="acc23")
 
-        cast_pairs(0, "v")
+        cast_pairs(0, "v", 0, 256)
+        cast_pairs(0, "v", 256, 512)
         cast_pairs(1, "s")
         gather_v(0)
         cast_pairs(2, "s")
@@ -193,20 +199,23 @@ def tile_routed_moe_kernel(tc, xT, w, gate, offs, out):
         cast_w(0, 2, 4, "s")
         weave(1, "wraw01")
         cast_w(1, 0, 2, "s")
-        quant_x(1, "wraw10")
         cast_w(1, 2, 4, "s")
         quant_w(0, 2)
-        mm(0, acc01[:, 0:C])
-        mm(1, acc01[:, C : 2 * C])
+        mm(0, acc0[:], 0, 2)
+        mm(1, acc1[:], 0, 2)
+        quant_x(1, "wraw11")
+        mm(0, acc0[:], 2, 4)
+        mm(1, acc1[:], 2, 4)
         cast_w(2, 0, 2, "s")
         cast_w(2, 2, 4, "s")
         cast_w(3, 0, 2, "s")
         quant_w(2, 3)
         mm(2, acc23[:, 0:C])
-        cast_w(3, 2, 4, "v")
+        cast_w(3, 2, 3, "s")
+        cast_w(3, 3, 4, "v")
         quant_w(3, 4)
         mm(3, acc23[:, C : 2 * C])
-        back(acc01, 0, 2 * C, "y01", "wraw31")
-        back(acc23, 2 * C, 2 * C, "y23", "y23")
+        back([acc0, acc1], 0, 2 * C, "y01", "wraw31")
+        back([acc23], 2 * C, 2 * C, "y23", "y23")
 
         nc.sync.dma_start(out=out, in_=window[:])

@@ -68,12 +68,12 @@ def tile_routed_moe_kernel(tc, xT, w, gate, offs, out):
         load_w(0, 2, 4)
         load_w(1, 0, 2)
         load_w(1, 2, 4)
-        load_gate()
         load_w(2, 0, 2)
         load_w(2, 2, 4)
         load_w(3, 0, 2)
         load_w(3, 2, 3)
         load_w(3, 3, 4)
+        load_gate()
 
         vwin = keep.tile([P, PAIRS * 2 * T], BF16, name="vwin")
         flat = {}

@@ -59,10 +59,8 @@ def tile_routed_moe_kernel(tc, xT, w, gate, offs, out):
         def load_gate():
             nc.sync.dma_start(out=gate_sb[:], in_=gate)
 
-        load_x_half(0, 0)
         load_offs()
-        load_x_half(0, 1)
-        for i in range(1, PAIRS):
+        for i in range(PAIRS):
             load_x(i)
         load_w(0, 0, 2)
         load_w(0, 2, 4)
@@ -176,8 +174,7 @@ def tile_routed_moe_kernel(tc, xT, w, gate, offs, out):
         acc1 = psum.tile([P, C], F32, name="acc1")
         acc23 = psum.tile([P, 2 * C], F32, name="acc23")
 
-        cast_pairs(0, "v", 0, 256)
-        cast_pairs(0, "v", 256, 512)
+        cast_pairs(0, "v")
         cast_pairs(1, "s")
         gather_v(0)
         cast_pairs(2, "s")

@@ -208,7 +208,7 @@ def tile_routed_moe_kernel(tc, xT, w, gate, offs, out):
         cast_w(3, 0, 2, "s")
         quant_w(2, 3)
         mm(2, acc23[:, 0:C])
-        cast_w(3, 2, 3, "s")
+        cast_w(3, 2, 3, "v")
         cast_w(3, 3, 4, "v")
         quant_w(3, 4)
         mm(3, acc23[:, C : 2 * C])

@@ -59,8 +59,9 @@ def tile_routed_moe_kernel(tc, xT, w, gate, offs, out):
         def load_gate():
             nc.sync.dma_start(out=gate_sb[:], in_=gate)
 
+        load_x(0)
         load_offs()
-        for i in range(PAIRS):
+        for i in range(1, PAIRS):
             load_x(i)
         load_w(0, 0, 2)
         load_w(0, 2, 4)
@@ -73,7 +74,8 @@ def tile_routed_moe_kernel(tc, xT, w, gate, offs, out):
         load_w(3, 3, 4)
         load_gate()
 
-        vwin = keep.tile([P, PAIRS * 2 * T], BF16, name="vwin")
+        vwin = keep.tile([P, (PAIRS + 1) * 2 * T], BF16, name="vwin")
+        nc.vector.memset(vwin[:, PAIRS * 2 * T :], 0.0)
         flat = {}
         for d in range(2):
             flat[d] = keep.tile([P, 4 * S], U32, name="flat%d" % d)
@@ -108,14 +110,7 @@ def tile_routed_moe_kernel(tc, xT, w, gate, offs, out):
             words = flat[i // 4][:, (i % 4) * S : (i % 4 + 1) * S]
             vw = vwin[:].bitcast(U32)
             c0 = pos(i) * T
-            if i == 0:
-                for h in range(2):
-                    nc.vector.tensor_copy(
-                        out=words[:, h * 256 : (h + 1) * 256],
-                        in_=vw[:, c0 : c0 + T].indirect(offsets[:, h * 16 : (h + 1) * 16]),
-                    )
-            else:
-                nc.vector.tensor_copy(out=words, in_=vw[:, c0 : c0 + 2 * T].indirect(offsets[:]))
+            nc.vector.tensor_copy(out=words, in_=vw[:, c0 : c0 + 2 * T].indirect(offsets[:]))
 
         def weave(d, tag):
             x_grouped[d] = keep.tile([P, 8 * S], BF16, name="xgrp%d" % d, tag=tag, align_bytes=64)
@@ -174,9 +169,11 @@ def tile_routed_moe_kernel(tc, xT, w, gate, offs, out):
         acc1 = psum.tile([P, C], F32, name="acc1")
         acc23 = psum.tile([P, 2 * C], F32, name="acc23")
 
-        cast_pairs(0, "v")
-        cast_pairs(1, "s")
+        cast_pairs(0, "v", 0, 352)
+        cast_pairs(0, "s", 352, T)
+        cast_pairs(1, "s", 0, 352)
         gather_v(0)
+        cast_pairs(1, "v", 352, T)
         cast_pairs(2, "s")
         gather_v(1)
         cast_pairs(3, "s")

@@ -125,8 +125,9 @@ def tile_routed_moe_kernel(tc, xT, w, gate, offs, out):
 
         def cast_w(e, g0, g1, eng):
             b = (e % 2) * PASSES
-            dst = w_grouped[e // 2][:].rearrange("p (g c i j) -> p g c j i", g=2 * PASSES, i=4, j=4)
-            src = w_raw[(e, g0 // 2)][:].rearrange("p g (j c i) -> p g c j i", j=4, i=4)
+            run = 4 if eng == "v" else 8
+            dst = w_grouped[e // 2][:].rearrange("p (g c i j) -> p g c j i", g=2 * PASSES, i=run, j=4)
+            src = w_raw[(e, g0 // 2)][:].rearrange("p g (j c i) -> p g c j i", j=4, i=run)
             cast(eng, dst[:, b + g0 : b + g1], src[:, g0 % 2 : g0 % 2 + g1 - g0])
 
         def quant_w(e0, e1):
@@ -205,7 +206,7 @@ def tile_routed_moe_kernel(tc, xT, w, gate, offs, out):
         cast_w(3, 0, 2, "s")
         quant_w(2, 3)
         mm(2, acc23[:, 0:C])
-        cast_w(3, 2, 3, "v")
+        cast_w(3, 2, 3, "s")
         cast_w(3, 3, 4, "v")
         quant_w(3, 4)
         mm(3, acc23[:, C : 2 * C])

@@ -130,10 +130,10 @@ def tile_routed_moe_kernel(tc, xT, w, gate, offs, out):
             src = w_raw[(e, g0 // 2)][:].rearrange("p g (j c i) -> p g c j i", j=4, i=run)
             cast(eng, dst[:, b + g0 : b + g1], src[:, g0 % 2 : g0 % 2 + g1 - g0])
 
-        def quant_w(e0, e1):
+        def quant_w(e0, e1, g0=0, g1=PASSES):
             q = e0 // 2
-            a = (e0 % 2) * PASSES
-            b = (e1 - 2 * q) * PASSES
+            a = (e0 % 2) * PASSES + g0
+            b = (e1 - 1 - 2 * q) * PASSES + g1
             nc.vector.quantize_mx(
                 out=w_codes[q][:, a * N : b * N].bitcast(FP8X4),
                 scales=w_scales[q][:, a * N : b * N],
@@ -208,7 +208,9 @@ def tile_routed_moe_kernel(tc, xT, w, gate, offs, out):
         mm(2, acc23[:, 0:C])
         cast_w(3, 2, 3, "s")
         cast_w(3, 3, 4, "v")
-        quant_w(3, 4)
+        quant_w(3, 4, 0, 2)
+        quant_w(3, 4, 2, 3)
+        quant_w(3, 4, 3, 4)
         mm(3, acc23[:, C : 2 * C])
         back([acc0, acc1], 0, 2 * C, "y01", "wraw31")
         back([acc23], 2 * C, 2 * C, "y23", "y23")

@@ -40,8 +40,10 @@ def tile_routed_moe_kernel(tc, xT, w, gate, offs, out):
             x_raw[i] = keep.tile([P, 2, T], F32, name="xraw%d" % i, align_bytes=64)
         w_raw = {}
         for e in range(E):
-            for h in range(2):
+            for h in range(1 if e == 3 else 2):
                 w_raw[(e, h)] = keep.tile([P, 2, 4 * N], F32, name="wraw%d%d" % (e, h), align_bytes=64)
+        for h in (2, 3):
+            w_raw[(3, h)] = keep.tile([P, 1, 4 * N], F32, name="wraw3%d" % h, align_bytes=64)
         gate_sb = keep.tile([P, S], F32, name="gate_sb")
 
         def load_offs():
@@ -53,8 +55,11 @@ def tile_routed_moe_kernel(tc, xT, w, gate, offs, out):
         def load_x_half(i, h):
             nc.sync.dma_start(out=x_raw[i][:, :, h * 256 : (h + 1) * 256], in_=x_view[i // 2, i % 2][:, :, h * 256 : (h + 1) * 256])
 
+        def raw_of(e, g0):
+            return w_raw[(e, g0)] if e == 3 and g0 >= 2 else w_raw[(e, g0 // 2)]
+
         def load_w(e, g0, g1):
-            nc.sync.dma_start(out=w_raw[(e, g0 // 2)][:, g0 % 2 : g0 % 2 + g1 - g0], in_=w_view[e][:, g0:g1])
+            nc.sync.dma_start(out=raw_of(e, g0)[:, g0 % 2 : g0 % 2 + g1 - g0] if g1 - g0 == 2 else raw_of(e, g0)[:], in_=w_view[e][:, g0:g1])
 
         def load_gate():
             nc.sync.dma_start(out=gate_sb[:], in_=gate)
@@ -127,8 +132,8 @@ def tile_routed_moe_kernel(tc, xT, w, gate, offs, out):
             b = (e % 2) * PASSES
             run = 4 if eng == "v" else 8
             dst = w_grouped[e // 2][:].rearrange("p (g c i j) -> p g c j i", g=2 * PASSES, i=run, j=4)
-            src = w_raw[(e, g0 // 2)][:].rearrange("p g (j c i) -> p g c j i", j=4, i=run)
-            cast(eng, dst[:, b + g0 : b + g1], src[:, g0 % 2 : g0 % 2 + g1 - g0])
+            src = raw_of(e, g0)[:].rearrange("p g (j c i) -> p g c j i", j=4, i=run)
+            cast(eng, dst[:, b + g0 : b + g1], src)
 
         def quant_w(e0, e1, g0=0, g1=PASSES):
             q = e0 // 2
@@ -166,8 +171,7 @@ def tile_routed_moe_kernel(tc, xT, w, gate, offs, out):
                 op=mult,
             )
 
-        acc0 = psum.tile([P, C], F32, name="acc0")
-        acc1 = psum.tile([P, C], F32, name="acc1")
+        acc01 = psum.tile([P, 2 * C], F32, name="acc01")
         acc23 = psum.tile([P, 2 * C], F32, name="acc23")
 
         cast_pairs(0, "v", 0, 352)
@@ -196,11 +200,9 @@ def tile_routed_moe_kernel(tc, xT, w, gate, offs, out):
         cast_w(1, 0, 2, "s")
         cast_w(1, 2, 4, "s")
         quant_w(0, 2)
-        mm(0, acc0[:], 0, 2)
-        mm(1, acc1[:], 0, 2)
         quant_x(1, "wraw11")
-        mm(0, acc0[:], 2, 4)
-        mm(1, acc1[:], 2, 4)
+        mm(0, acc01[:, 0:C])
+        mm(1, acc01[:, C : 2 * C])
         cast_w(2, 0, 2, "s")
         cast_w(2, 2, 4, "s")
         cast_w(3, 0, 2, "s")
@@ -212,7 +214,7 @@ def tile_routed_moe_kernel(tc, xT, w, gate, offs, out):
         quant_w(3, 4, 2, 3)
         quant_w(3, 4, 3, 4)
         mm(3, acc23[:, C : 2 * C])
-        back([acc0, acc1], 0, 2 * C, "y01", "wraw31")
+        back([acc01], 0, 2 * C, "y01", "wraw32")
         back([acc23], 2 * C, 2 * C, "y23", "y23")
 
         nc.sync.dma_start(out=out, in_=window[:])

@@ -119,7 +119,7 @@ def tile_routed_moe_kernel(tc, xT, w, gate, offs, out):
 
         def weave(d, tag):
             x_grouped[d] = keep.tile([P, 8 * S], BF16, name="xgrp%d" % d, tag=tag, align_bytes=64)
-            nc.vector.tensor_copy(
+            (nc.gpsimd if d == 0 else nc.vector).tensor_copy(
                 out=x_grouped[d][:].bitcast(I32).rearrange("p (g s u) -> p g s u", g=2, u=2),
                 in_=flat[d][:].bitcast(I32).rearrange("p (g u s) -> p g s u", g=2, u=2),
             )
@@ -186,8 +186,8 @@ def tile_routed_moe_kernel(tc, xT, w, gate, offs, out):
         cast_pairs(4, "s")
         gather_v(3)
         cast_pairs(5, "s")
+        weave(0, "xgrp0")
         gather_v(4)
-        weave(0, "xraw5")
         gather_v(5)
         cast_pairs(6, "s")
         gather_v(6)
@@ -208,13 +208,12 @@ def tile_routed_moe_kernel(tc, xT, w, gate, offs, out):
         cast_w(3, 0, 2, "s")
         quant_w(2, 3)
         mm(2, acc23[:, 0:C])
-        cast_w(3, 2, 3, "s")
+        cast_w(3, 2, 3, "v")
         cast_w(3, 3, 4, "v")
+        quant_w(3, 4, 2, 4)
         quant_w(3, 4, 0, 2)
-        quant_w(3, 4, 2, 3)
-        quant_w(3, 4, 3, 4)
         mm(3, acc23[:, C : 2 * C])
-        back([acc01], 0, 2 * C, "y01", "wraw32")
+        back([acc01], 0, 2 * C, "y01", "wraw30")
         back([acc23], 2 * C, 2 * C, "y23", "y23")
 
         nc.sync.dma_start(out=out, in_=window[:])

from contextlib import ExitStack

import concourse.mybir as mybir

K, T, E, C, N = 2048, 512, 4, 128, 128
FLOPS = 2 * K * N * E * C

F32 = mybir.dt.float32
BF16 = mybir.dt.bfloat16
U32 = mybir.dt.uint32
U16 = mybir.dt.uint16
U8 = mybir.dt.uint8
I32 = mybir.dt.int32
FP8X4 = mybir.dt.float8_e4m3fn_x4

P = 128
PASSES = K // 512
S = E * C
PAIRS = 2 * PASSES


def tile_routed_moe_kernel(tc, xT, w, gate, offs, out):
    nc = tc.nc
    mult = mybir.AluOpType.mult

    with ExitStack() as ctx:
        keep = ctx.enter_context(tc.tile_pool(name="keep", bufs=1))
        psum = ctx.enter_context(tc.psum_pool(name="psum", bufs=1))

        offsets = keep.tile([P, S // 16], U16, name="offsets")
        warm_in = keep.tile([P, 8], F32, name="warm_in")
        warm_out = keep.tile([P, 8], F32, name="warm_out")
        nc.vector.memset(warm_in[:], 0.0)
        nc.scalar.copy(out=warm_out[:], in_=warm_in[:])

        x_view = xT.rearrange("(g p u e) n -> g u p e n", p=P, u=2, e=2)
        w_view = w.rearrange("e (g p j) n -> e p g (j n)", p=P, j=4)
        x_raw = {}
        for i in range(PAIRS):
            x_raw[i] = keep.tile([P, 2, T], F32, name="xraw%d" % i, align_bytes=64)
        w_raw = {}
        for e in range(E):
            for h in range(1 if e == 3 else 2):
                w_raw[(e, h)] = keep.tile([P, 2, 4 * N], F32, name="wraw%d%d" % (e, h), align_bytes=64)
        for h in (2, 3):
            w_raw[(3, h)] = keep.tile([P, 1, 4 * N], F32, name="wraw3%d" % h, align_bytes=64)
        gate_sb = keep.tile([P, S], F32, name="gate_sb")

        def load_offs():
            nc.sync.dma_start(offsets[:], offs)

        def load_x(i):
            nc.sync.dma_start(out=x_raw[i][:], in_=x_view[i // 2, i % 2])

        def load_x_half(i, h):
            nc.sync.dma_start(out=x_raw[i][:, :, h * 256 : (h + 1) * 256], in_=x_view[i // 2, i % 2][:, :, h * 256 : (h + 1) * 256])

        def raw_of(e, g0):
            return w_raw[(e, g0)] if e == 3 and g0 >= 2 else w_raw[(e, g0 // 2)]

        def load_w(e, g0, g1):
            nc.sync.dma_start(out=raw_of(e, g0)[:, g0 % 2 : g0 % 2 + g1 - g0] if g1 - g0 == 2 else raw_of(e, g0)[:], in_=w_view[e][:, g0:g1])

        def load_gate():
            nc.sync.dma_start(out=gate_sb[:], in_=gate)

        load_x(0)
        load_offs()
        for i in range(1, PAIRS):
            load_x(i)
        load_w(0, 0, 2)
        load_w(0, 2, 4)
        load_w(1, 0, 2)
        load_w(1, 2, 4)
        load_w(2, 0, 2)
        load_w(2, 2, 4)
        load_w(3, 0, 2)
        load_w(3, 2, 3)
        load_w(3, 3, 4)
        load_gate()

        vwin = keep.tile([P, (PAIRS + 1) * 2 * T], BF16, name="vwin")
        nc.vector.memset(vwin[:, PAIRS * 2 * T :], 0.0)
        flat = {}
        for d in range(2):
            flat[d] = keep.tile([P, 4 * S], U32, name="flat%d" % d)
        x_grouped = {}
        x_codes = {}
        x_scales = {}
        for d in range(2):
            x_scales[d] = keep.tile([P, 2 * S], U8, name="xscales%d" % d, align_bytes=64)
        w_grouped = {}
        w_codes = {}
        w_scales = {}
        for q in range(2):
            w_grouped[q] = keep.tile([P, 2 * PASSES * 4 * N], BF16, name="wgrp%d" % q, align_bytes=64)
            w_codes[q] = keep.tile([P, 2 * PASSES * N], U32, name="wcodes%d" % q, align_bytes=64)
            w_scales[q] = keep.tile([P, 2 * PASSES * N], U8, name="wscales%d" % q, align_bytes=64)
        window = keep.tile([P, T], F32, name="window")

        def cast(eng, dst, src):
            if eng == "v":
                nc.vector.tensor_copy(out=dst, in_=src)
            else:
                nc.scalar.copy(out=dst, in_=src)

        def pos(i):
            return PAIRS - 1 - i

        def cast_pairs(i, eng, n0=0, n1=T):
            dst = vwin[:, pos(i) * 2 * T : (pos(i) + 1) * 2 * T].rearrange("p (n e) -> p n e", e=2)
            cast(eng, dst[:, n0:n1], x_raw[i][:, :, n0:n1].rearrange("p e n -> p n e"))

        def gather_v(i):
            words = flat[i // 4][:, (i % 4) * S : (i % 4 + 1) * S]
            vw = vwin[:].bitcast(U32)
            c0 = pos(i) * T
            nc.vector.tensor_copy(out=words, in_=vw[:, c0 : c0 + 2 * T].indirect(offsets[:]))

        def weave(d, tag):
            x_grouped[d] = keep.tile([P, 8 * S], BF16, name="xgrp%d" % d, tag=tag, align_bytes=64)
            (nc.gpsimd if d == 0 else nc.vector).tensor_copy(
                out=x_grouped[d][:].bitcast(I32).rearrange("p (g s u) -> p g s u", g=2, u=2),
                in_=flat[d][:].bitcast(I32).rearrange("p (g u s) -> p g s u", g=2, u=2),
            )

        def quant_x(d, tag):
            x_codes[d] = keep.tile([P, 2 * S], U32, name="xcodes%d" % d, tag=tag, align_bytes=64)
            nc.vector.quantize_mx(out=x_codes[d][:].bitcast(FP8X4), scales=x_scales[d][:], in_=x_grouped[d][:])

        def cast_w(e, g0, g1, eng):
            b = (e % 2) * PASSES
            run = 4 if eng == "v" else 8
            dst = w_grouped[e // 2][:].rearrange("p (g c i j) -> p g c j i", g=2 * PASSES, i=run, j=4)
            src = raw_of(e, g0)[:].rearrange("p g (j c i) -> p g c j i", j=4, i=run)
            cast(eng, dst[:, b + g0 : b + g1], src)

        def quant_w(e0, e1, g0=0, g1=PASSES):
            q = e0 // 2
            a = (e0 % 2) * PASSES + g0
            b = (e1 - 1 - 2 * q) * PASSES + g1
            nc.vector.quantize_mx(
                out=w_codes[q][:, a * N : b * N].bitcast(FP8X4),
                scales=w_scales[q][:, a * N : b * N],
                in_=w_grouped[q][:, a * 4 * N : b * 4 * N],
            )

        def mm(e, acc, g0=0, g1=PASSES):
            for g in range(g0, g1):
                c0 = ((e % 2) * PASSES + g) * N
                r0 = (g % 2) * S + e * C
                nc.tensor.matmul_mx(
                    out=acc,
                    lhsT=w_codes[e // 2][:, c0 : c0 + N].bitcast(FP8X4),
                    lhsT_scale=w_scales[e // 2][:, c0 : c0 + N],
                    rhs=x_codes[g // 2][:, r0 : r0 + C].bitcast(FP8X4),
                    rhs_scale=x_scales[g // 2][:, r0 : r0 + C],
                    start=(g == 0),
                    stop=(g == PASSES - 1),
                )

        def back(accs, s0, n, name, tag):
            y = keep.tile([P, n], F32, name=name, tag=tag, align_bytes=64)
            m = n // len(accs)
            for a, acc in enumerate(accs):
                nc.scalar.copy(out=y[:, a * m : (a + 1) * m], in_=acc[:])
            nc.vector.tensor_tensor(
                out=window[:].indirect(offsets[:, s0 // 16 : (s0 + n) // 16]),
                in0=y[:],
                in1=gate_sb[:, s0 : s0 + n],
                op=mult,
            )

        acc01 = psum.tile([P, 2 * C], F32, name="acc01")
        acc23 = psum.tile([P, 2 * C], F32, name="acc23")

        cast_pairs(0, "v", 0, 352)
        cast_pairs(0, "s", 352, T)
        cast_pairs(1, "s", 0, 352)
        gather_v(0)
        cast_pairs(1, "v", 352, T)
        cast_pairs(2, "s")
        gather_v(1)
        cast_pairs(3, "s")
        gather_v(2)
        cast_pairs(4, "s")
        gather_v(3)
        cast_pairs(5, "s")
        weave(0, "xgrp0")
        gather_v(4)
        gather_v(5)
        cast_pairs(6, "s")
        gather_v(6)
        cast_pairs(7, "s")
        gather_v(7)
        cast_w(0, 0, 2, "s")
        quant_x(0, "wraw00")
        cast_w(0, 2, 4, "s")
        weave(1, "wraw01")
        cast_w(1, 0, 2, "s")
        cast_w(1, 2, 4, "s")
        quant_w(0, 2)
        quant_x(1, "wraw11")
        mm(0, acc01[:, 0:C])
        mm(1, acc01[:, C : 2 * C])
        cast_w(2, 0, 2, "s")
        cast_w(2, 2, 4, "s")
        cast_w(3, 0, 2, "s")
        quant_w(2, 3)
        mm(2, acc23[:, 0:C])
        cast_w(3, 2, 3, "v")
        cast_w(3, 3, 4, "v")
        quant_w(3, 4, 2, 4)
        quant_w(3, 4, 0, 2)
        mm(3, acc23[:, C : 2 * C])
        back([acc01], 0, 2 * C, "y01", "wraw30")
        back([acc23], 2 * C, 2 * C, "y23", "y23")

        nc.sync.dma_start(out=out, in_=window[:])
